import numpy as np
import ml_dtypes


def mxq(x, axis, fmt="e4m3"):
    dtype, down = {"e4m3": (ml_dtypes.float8_e4m3fn, 7), "e5m2": (ml_dtypes.float8_e5m2, 14)}[fmt]
    v = np.moveaxis(np.asarray(x, np.float32).astype(ml_dtypes.bfloat16).astype(np.float64), axis, -1)
    blocks = v.reshape(v.shape[:-1] + (-1, 32))
    amax = np.abs(blocks).max(-1, keepdims=True)
    byte = np.maximum(np.where(amax > 0, np.frexp(amax)[1] - 1 + 127, 0) - down, 1)
    scale = np.exp2(byte - 127.0)
    codes = (blocks / scale).astype(np.float32).astype(dtype).astype(np.float64)
    return np.moveaxis((codes * scale).reshape(v.shape), -1, axis)


WIDE = False


def mx_kscale(k):
    if not WIDE:
        return np.ones(k)
    levels = np.array([10, -10, 5, -5, 0])
    if k % 512:
        return np.exp2(np.random.permutation(np.resize(levels, k // 32))).repeat(32)
    a = np.empty((k // 512, 16))
    for p in range(k // 512):
        a[p, :8] = np.random.permutation(np.resize(levels, 8))
        for g in range(8):
            far = levels[np.abs(levels - a[p, g]) >= 10]
            a[p, g + 8] = far[np.random.randint(len(far))]
    return np.exp2(a.ravel()).repeat(32)


def f64(x):
    return np.asarray(x).astype(np.float64)


def striped(idx):
    return np.tile(idx.reshape(-1, 16).T, (8, 1)).astype(np.uint16)


def unstriped(offs):
    return offs[:16].T.reshape(-1).astype(np.int64)


def striped8(idx):
    return np.concatenate([x.reshape(-1, 16).T for x in idx]).astype(np.uint16)


def runs(offs, k):
    lists = np.stack([offs[16 * r : 16 * r + 16].T.reshape(-1) for r in range(8)]).astype(np.int64)
    return lists[np.arange(k) % 512 // 64]


def pack_weight(w):
    k, n = w.shape
    w = f64(np.asarray(w, np.float32).astype(ml_dtypes.bfloat16)).reshape(k // 32, 32, n)
    amax = np.abs(w).max(1)
    byte = np.clip(np.where(amax > 0, np.frexp(amax)[1] - 1 + 127 - 7, 1), 1, 254)
    scaled = (w * np.exp2(127.0 - byte)[:, None, :]).reshape(k, n).astype(np.float32)
    words = np.ascontiguousarray(scaled.reshape(k // 512, 128, 4, n).transpose(0, 1, 3, 2)).astype(ml_dtypes.float8_e4m3fn).view(np.uint8)
    return words, np.ascontiguousarray(byte.astype(np.uint8).reshape(k // 512, 16, n))


def unpack_weight(words, scales):
    g, p, n, _ = words.shape
    vals = np.ascontiguousarray(words).view(ml_dtypes.float8_e4m3fn).astype(np.float64) * np.repeat(np.exp2(scales.astype(np.float64) - 127.0), 8, axis=1)[..., None]
    return vals.transpose(0, 1, 3, 2).reshape(g * 512, n)


E2M1 = np.array([0.0, 0.5, 1.0, 1.5, 2.0, 3.0, 4.0, 6.0, -0.0, -0.5, -1.0, -1.5, -2.0, -3.0, -4.0, -6.0])


def pack_fp4(w):
    k, n = w.shape
    w = f64(np.asarray(w, np.float32).astype(ml_dtypes.bfloat16)).reshape(k // 32, 32, n)
    amax = np.abs(w).max(1)
    mant, ex = np.frexp(amax / 6.0)
    byte = np.clip(np.where(amax > 0, np.where(mant > 0.5, ex, ex - 1) + 127, 1), 1, 254)
    scaled = (w * np.exp2(127.0 - byte)[:, None, :]).reshape(k, n).astype(np.float32)
    c = np.ascontiguousarray(scaled.reshape(k // 512, 128, 4, n).transpose(0, 1, 3, 2)).astype(ml_dtypes.float4_e2m1fn).view(np.uint8) & 0xF
    words = (c[..., 0::2] | (c[..., 1::2] << 4)).reshape(k // 512, 128, 2 * n)
    return np.ascontiguousarray(words), np.ascontiguousarray(byte.astype(np.uint8).reshape(k // 512, 16, n))


def unpack_fp4(words, scales):
    g, _, n = scales.shape
    words = np.ascontiguousarray(words).reshape(g, 128, n, 2)
    nib = np.empty((g, 128, n, 4), np.uint8)
    nib[..., 0::2] = words & 0xF
    nib[..., 1::2] = words >> 4
    vals = E2M1[nib] * np.repeat(np.exp2(scales.astype(np.float64) - 127.0), 8, axis=1)[..., None]
    return vals.transpose(0, 1, 3, 2).reshape(g * 512, n)


def sigmoid(v):
    return 1.0 / (1.0 + np.exp(-np.maximum(v, -700.0)))

def planes(y):
    n, m = y.shape
    v = y.astype(np.float32).astype(ml_dtypes.bfloat16).astype(np.float64).reshape(n // 32, 32, m)
    top = np.abs(v).max(1)
    byte = np.clip(np.where(top > 0, np.frexp(top)[1] - 1 + 127 - 7, 1), 1, 254)
    codes = (v * np.exp2(127.0 - byte)[:, None, :]).reshape(n, m).astype(np.float32).astype(ml_dtypes.float8_e4m3fn).view(np.uint8)
    words = codes.reshape(n // 512, 128, 4, m).transpose(0, 1, 3, 2)
    return np.ascontiguousarray(words), np.ascontiguousarray(byte.astype(np.uint8).reshape(n // 512, 16, m))


K, T, S, N, H = 512, 2048, 512, 512, 512


def setup_inputs():
    n = np.random.standard_normal
    s = mx_kscale(K)[:, None]
    u = mx_kscale(H)
    packed_xT = pack_weight(n((K, T)) * s)
    packed_w1 = pack_fp4(n((K, H)) / np.sqrt(K) / s)
    packed_w2 = pack_fp4(n((H, N)) / np.sqrt(H) / u[:, None])
    return {
        "x_words": packed_xT[0],
        "x_scales": packed_xT[1],
        "w1_words": packed_w1[0],
        "w1_scales": packed_w1[1],
        "gn": (np.random.uniform(0.5, 1.5, (H, 1)) * u[:, None]).astype(np.float32),
        "w2_words": packed_w2[0],
        "w2_scales": packed_w2[1],
        "offs": striped(np.random.permutation(T)[:S]),
        "n1": striped8(np.stack([np.random.permutation(S) for _ in range(8)])),
        "n2": striped8(np.stack([np.random.permutation(S) for _ in range(8)])),
    }


def reference(x_words, x_scales, w1_words, w1_scales, gn, w2_words, w2_scales, offs, n1, n2):
    xq = unpack_weight(x_words, x_scales)[:, unstriped(offs)]
    y = sigmoid(unpack_fp4(w1_words, w1_scales).T @ xq)
    lm = 3.5 * (y * (-1.0 * y + 1))
    z = f64(gn) * (0.6 * lm - (0.4 * (lm[np.arange(H)[:, None], runs(n1, H)] + lm[np.arange(H)[:, None], runs(n2, H)])))
    out_0 = unpack_fp4(w2_words, w2_scales).T @ mxq(z, 0, "e4m3")
    return (out_0,) + planes(out_0)

@@ -1,0 +1,236 @@
+from contextlib import ExitStack
+
+import concourse.mybir as mybir
+
+K, T, S, N, H = 512, 2048, 512, 512, 512
+FLOPS = 2 * K * H * S + 2 * H * N * S
+
+F32 = mybir.dt.float32
+BF16 = mybir.dt.bfloat16
+I32 = mybir.dt.int32
+U32 = mybir.dt.uint32
+U16 = mybir.dt.uint16
+U8 = mybir.dt.uint8
+FP8X4 = mybir.dt.float8_e4m3fn_x4
+FP4X4 = mybir.dt.float4_e2m1fn_x4
+ACT = mybir.ActivationFunctionType
+ALU = mybir.AluOpType
+
+P = 128
+PACK = 4
+BLK = 128
+NBLK = S // BLK
+HALF = S // 2
+
+
+def tile_picked_cmlmap_none_po_kernel(tc, x_words, x_scales, w1_words, w1_scales, gn, w2_words, w2_scales, offs, n1, n2, out_0, out_1, out_2):
+    nc = tc.nc
+    with ExitStack() as ctx:
+        lists = ctx.enter_context(tc.tile_pool(name="lists", bufs=1))
+        keep = ctx.enter_context(tc.tile_pool(name="keep", bufs=1))
+        psum = ctx.enter_context(tc.psum_pool(name="psum", bufs=1))
+
+        offs_t = lists.tile([P, S // 16], U16, name="offs_t")
+        n1_t = lists.tile([P, S // 16], U16, name="n1_t")
+        n2_t = lists.tile([P, S // 16], U16, name="n2_t")
+
+        xw = keep.tile([P, T], I32, name="xw", tag="xw", align_bytes=64)
+        xs = keep.tile([P, T], U8, name="xs", align_bytes=64)
+        w1r = keep.tile([P, 2 * H], U8, name="w1r", tag="w1r", align_bytes=64)
+        w2r = keep.tile([P, 2 * N], U8, name="w2r", align_bytes=64)
+        s1r = keep.tile([P, H], U8, name="s1r", align_bytes=64)
+        gain = keep.tile([P, PACK], F32, name="gain")
+        warm = keep.tile([P, 1], F32, name="warm")
+        warm2 = keep.tile([P, 1], F32, name="warm2")
+
+        nc.vector.memset(s1r[:].bitcast(I32), 0)
+        nc.vector.memset(xs[:].bitcast(I32), 0)
+        nc.gpsimd.memset(warm[:], 0.0)
+
+        def load_scales(eng, tile, src, q):
+            eng.dma_start(out=tile[32 * q : 32 * q + 4, :].bitcast(I32), in_=src[0, 4 * q : 4 * q + 4, :].bitcast(I32))
+
+        nc.sync.dma_start(out=w1r[:].bitcast(I32), in_=w1_words[0].bitcast(I32))
+        nc.sync.dma_start(offs_t[:], offs)
+        nc.sync.dma_start(n1_t[:], n1)
+        nc.sync.dma_start(n2_t[:], n2)
+        nc.sync.dma_start(out=gain[:], in_=gn.rearrange("(p t) o -> p (t o)", t=PACK))
+        nc.sync.dma_start(out=xw[:], in_=x_words[0].rearrange("p c r -> p (c r)").bitcast(I32))
+        nc.sync.dma_start(out=w2r[:].bitcast(I32), in_=w2_words[0].bitcast(I32))
+        nc.scalar.activation(out=warm2[:], in_=warm[:], func=ACT.Tanh)
+        for q in range(4):
+            load_scales(nc.scalar, s1r, w1_scales, q)
+        for q in range(4):
+            load_scales(nc.scalar if q < 2 else nc.gpsimd, xs, x_scales, q)
+
+        def deal_words(dst, src):
+            nc.vector.tensor_copy(
+                out=dst[:].rearrange("p (t m b) -> p t m b", t=PACK, b=2),
+                in_=src[:].rearrange("p (m t b) -> p t m b", t=PACK, b=2),
+            )
+
+        def deal_scales(dst, src):
+            nc.vector.tensor_copy(
+                out=dst[:].rearrange("p (t m) -> p t m", t=PACK),
+                in_=src[:].rearrange("p (m t) -> p t m", t=PACK),
+            )
+
+        w1d = keep.tile([P, 2 * H], U8, name="w1d", align_bytes=64)
+        s1d = keep.tile([P, H], U8, name="s1d", align_bytes=64)
+        deal_words(w1d, w1r)
+        deal_scales(s1d, s1r)
+
+        s2r = keep.tile([P, N], U8, name="s2r", tag="w1r", align_bytes=64)
+        nc.gpsimd.memset(s2r[:].bitcast(I32), 0)
+        for q in range(4):
+            load_scales(nc.sync, s2r, w2_scales, q)
+
+        xg = keep.tile([P, S], U32, name="xg", align_bytes=64)
+        xgs = keep.tile([P, S], U8, name="xgs", align_bytes=64)
+        nc.vector.tensor_copy(xgs[:], xs[:].indirect(offs_t[:]))
+        for h in range(2):
+            nc.vector.tensor_copy(xg[:, HALF * h : HALF * (h + 1)], xw[:].bitcast(U32).indirect(offs_t[:, 16 * h : 16 * (h + 1)]))
+
+        coef = keep.tile([P, 4, PACK], F32, name="coef")
+        for i, v in enumerate((0.35, -0.35, -0.525, 0.525)):
+            nc.gpsimd.tensor_scalar(coef[:, i, :], gain[:], v, 0.0, ALU.mult, ALU.add)
+
+        w2d = keep.tile([P, 2 * N], U8, name="w2d", tag="xw", align_bytes=64)
+        s2d = keep.tile([P, N], U8, name="s2d", align_bytes=64)
+
+        wide = [keep.tile([P, 2 * S], F32, name=f"wide{t}") for t in range(2)]
+        narrow = [keep.tile([P, S], F32, name=f"narrow{t}") for t in range(2)]
+        win = wide + narrow
+        nb = [w[:, 0:S] for w in win]
+        own = [keep.tile([P, S], F32, name=f"own{t}") for t in range(PACK)]
+        th23 = [keep.tile([P, S], F32, name=f"th{t}") for t in range(2)]
+        th = [w[:, S : 2 * S] for w in wide] + [x[:] for x in th23]
+        sq = [keep.tile([P, S], F32, name=f"sq{t}") for t in range(PACK)]
+
+        def layer1(t, cols, name):
+            u = psum.tile([P, cols.stop - cols.start], F32, name=name, tag=name)
+            nc.tensor.matmul_mx(
+                out=u[:],
+                lhsT=w1d[:, 2 * P * t : 2 * P * (t + 1)].bitcast(FP4X4),
+                lhsT_scale=s1d[:, P * t : P * (t + 1)],
+                rhs=xg[:, cols].bitcast(FP8X4),
+                rhs_scale=xgs[:, cols],
+                start=True,
+                stop=True,
+            )
+            nc.scalar.activation(out=th[t][:, cols], in_=u[:], func=ACT.Tanh, scale=0.5)
+            nc.scalar.activation(out=sq[t][:, cols], in_=th[t][:, cols], func=ACT.Square)
+
+        def affine_scalar(dst, t, cols, i):
+            nc.scalar.activation(out=dst[t][:, cols], in_=sq[t][:, cols], func=ACT.Identity, scale=coef[:, i, t : t + 1], bias=coef[:, i + 1, t : t + 1])
+
+        halves = (slice(0, HALF), slice(HALF, S))
+        for h in range(2):
+            layer1(0, halves[h], f"bank{h}")
+            nc.vector.tensor_scalar(nb[0][:, halves[h]], sq[0][:, halves[h]], coef[:, 0, 0:1], coef[:, 1, 0:1], ALU.mult, ALU.add)
+        for h in range(2):
+            affine_scalar(own, 0, halves[h], 2)
+        deal_words(w2d, w2r)
+        deal_scales(s2d, s2r)
+        for t in range(1, PACK):
+            layer1(t, slice(0, S), f"bank{t + 1}")
+            affine_scalar(nb, t, slice(0, S), 0)
+            affine_scalar(own, t, slice(0, S), 2)
+
+        full = keep.tile([P, PACK, S], F32, name="full")
+        parts = {}
+
+        def first(t, cols, tag):
+            dst = keep.tile([P, cols.stop - cols.start], F32, name=f"part{t}_{cols.start}", tag=tag, align_bytes=64)
+            parts[t] = (dst, cols.start)
+            nc.vector.tensor_tensor(dst[:], win[t][:].indirect(n1_t[:, cols.start // 16 : cols.stop // 16]), own[t][:, cols], ALU.add)
+
+        def second(t, cols):
+            src, base = parts[t]
+            nc.vector.tensor_tensor(full[:, t, cols], win[t][:].indirect(n2_t[:, cols.start // 16 : cols.stop // 16]), src[:, cols.start - base : cols.stop - base], ALU.add)
+
+        ow = keep.tile([P, S], U32, name="ow", align_bytes=64)
+        osc = keep.tile([P, S], U8, name="osc", align_bytes=64)
+        out_rows = out_0.rearrange("(p t) j -> p t j", t=PACK)
+        out_w = out_1[0].rearrange("p c r -> p (c r)").bitcast(I32)
+        zb = {}
+        acc = {}
+        o32 = {}
+        ob = {}
+
+        def blk(c):
+            return slice(BLK * c, BLK * (c + 1))
+
+        def round_z(c, copy):
+            zb[c] = keep.tile([P, BLK, PACK], BF16, name=f"zb{c}", tag=f"zb{c}", align_bytes=64)
+            copy(
+                out=zb[c][:].rearrange("p (a i) t -> p a t i", i=2),
+                in_=full[:, :, blk(c)].rearrange("p t (a i) -> p a t i", i=2),
+            )
+
+        def layer2(c, bank):
+            zw = keep.tile([P, BLK], U32, name=f"zw{c}", align_bytes=64)
+            zs = keep.tile([P, BLK], U8, name=f"zs{c}", align_bytes=64)
+            nc.vector.quantize_mx(out=zw[:].bitcast(FP8X4), scales=zs[:], in_=zb[c][:].rearrange("p j t -> p (j t)"))
+            acc[c] = psum.tile([P, PACK, BLK], F32, name=f"acc{c}", tag=bank)
+            for t in range(PACK):
+                nc.tensor.matmul_mx(
+                    out=acc[c][:, t, :],
+                    lhsT=w2d[:, 2 * P * t : 2 * P * (t + 1)].bitcast(FP4X4),
+                    lhsT_scale=s2d[:, P * t : P * (t + 1)],
+                    rhs=zw[:].bitcast(FP8X4),
+                    rhs_scale=zs[:],
+                    start=True,
+                    stop=True,
+                )
+
+        def store_f32(c):
+            o32[c] = keep.tile([P, PACK, BLK], F32, name=f"o32_{c}")
+            nc.scalar.copy(out=o32[c][:], in_=acc[c][:])
+            nc.sync.dma_start(out=out_rows[:, :, blk(c)], in_=o32[c][:])
+
+        def round_out(c, copy, src):
+            ob[c] = keep.tile([P, BLK, PACK], BF16, name=f"ob{c}", align_bytes=64)
+            copy(
+                out=ob[c][:].rearrange("p (a i) t -> p a t i", i=2),
+                in_=src[:].rearrange("p t (a i) -> p a t i", i=2),
+            )
+
+        def planes(c):
+            nc.vector.quantize_mx(out=ow[:, blk(c)].bitcast(FP8X4), scales=osc[:, blk(c)], in_=ob[c][:].rearrange("p j t -> p (j t)"))
+            nc.sync.dma_start(out=out_w[:, blk(c)], in_=ow[:, blk(c)].bitcast(I32))
+
+        whole = slice(0, S)
+        first(0, whole, "p0")
+        second(0, whole)
+        first(1, whole, "p1")
+        second(1, whole)
+        first(2, halves[0], "p2")
+        second(2, halves[0])
+        first(3, halves[0], "p3")
+        second(3, blk(0))
+        round_z(0, nc.scalar.copy)
+        second(3, blk(1))
+        round_z(1, nc.scalar.copy)
+        first(2, halves[1], "p3")
+        layer2(0, "bank5")
+        second(2, halves[1])
+        first(3, halves[1], "zb0")
+        layer2(1, "bank6")
+        second(3, blk(2))
+        round_z(2, nc.scalar.copy)
+        second(3, blk(3))
+        round_z(3, nc.vector.tensor_copy)
+        layer2(2, "bank7")
+        layer2(3, "bank0")
+        for c in (0, 1):
+            round_out(c, nc.scalar.copy, acc[c])
+            store_f32(c)
+            planes(c)
+        for c in (2, 3):
+            store_f32(c)
+            round_out(c, nc.vector.tensor_copy, o32[c])
+            planes(c)
+        for q in range(4):
+            eng = nc.scalar if q % 2 else nc.sync
+            eng.dma_start(out=out_2[0, 4 * q : 4 * q + 4, :].bitcast(I32), in_=osc[32 * q : 32 * q + 4, :].bitcast(I32))

@@ -34,110 +34,117 @@ def tile_picked_cmlmap_none_po_kernel(tc, x_words, x_scales, w1_words, w1_scales
         n1_t = lists.tile([P, S // 16], U16, name="n1_t")
         n2_t = lists.tile([P, S // 16], U16, name="n2_t")
 
-        xw = keep.tile([P, T], I32, name="xw", tag="xw", align_bytes=64)
-        xs = keep.tile([P, T], U8, name="xs", align_bytes=64)
-        w1r = keep.tile([P, 2 * H], U8, name="w1r", tag="w1r", align_bytes=64)
-        w2r = keep.tile([P, 2 * N], U8, name="w2r", align_bytes=64)
-        s1r = keep.tile([P, H], U8, name="s1r", align_bytes=64)
+        xs = keep.tile([P, T], U8, name="xs", tag="xs", align_bytes=64)
+        w1r = keep.tile([P, 2 * H], U8, name="w1r", align_bytes=64)
+        w2r = keep.tile([P, 2 * N], U8, name="w2r", tag="w2r", align_bytes=64)
+        s1r = keep.tile([P, H], U8, name="s1r", tag="s1r", align_bytes=64)
+        s2r = keep.tile([P, N], U8, name="s2r", tag="s2r", align_bytes=64)
         gain = keep.tile([P, PACK], F32, name="gain")
         warm = keep.tile([P, 1], F32, name="warm")
         warm2 = keep.tile([P, 1], F32, name="warm2")
+        blank = keep.tile([P, H // 4], I32, name="blank", tag="xw", align_bytes=64)
 
-        nc.vector.memset(s1r[:].bitcast(I32), 0)
         nc.vector.memset(xs[:].bitcast(I32), 0)
-        nc.gpsimd.memset(warm[:], 0.0)
+        nc.vector.memset(blank[:], 0)
+        nc.vector.tensor_copy(s1r[:].bitcast(I32), blank[:])
+        nc.vector.memset(warm[:], 0.0)
+        nc.vector.memset(s2r[:].bitcast(I32), 0)
+        xw = keep.tile([P, T], I32, name="xw", tag="xw", align_bytes=64)
 
         def load_scales(eng, tile, src, q):
             eng.dma_start(out=tile[32 * q : 32 * q + 4, :].bitcast(I32), in_=src[0, 4 * q : 4 * q + 4, :].bitcast(I32))
 
-        nc.sync.dma_start(out=w1r[:].bitcast(I32), in_=w1_words[0].bitcast(I32))
+        nc.gpsimd.dma_start(out=w1r[:].bitcast(I32), in_=w1_words[0].bitcast(I32))
+        load_scales(nc.gpsimd, s2r, w2_scales, 3)
+        nc.gpsimd.dma_start(out=gain[:], in_=gn.rearrange("(p t) o -> p (t o)", t=PACK))
+        nc.gpsimd.dma_start(out=w2r[:].bitcast(I32), in_=w2_words[0].bitcast(I32))
         nc.sync.dma_start(offs_t[:], offs)
         nc.sync.dma_start(n1_t[:], n1)
         nc.sync.dma_start(n2_t[:], n2)
-        nc.sync.dma_start(out=gain[:], in_=gn.rearrange("(p t) o -> p (t o)", t=PACK))
-        nc.sync.dma_start(out=xw[:], in_=x_words[0].rearrange("p c r -> p (c r)").bitcast(I32))
-        nc.sync.dma_start(out=w2r[:].bitcast(I32), in_=w2_words[0].bitcast(I32))
-        nc.scalar.activation(out=warm2[:], in_=warm[:], func=ACT.Tanh)
         for q in range(4):
-            load_scales(nc.scalar, s1r, w1_scales, q)
+            load_scales(nc.sync, xs, x_scales, q)
+        x_rows = x_words[0].rearrange("p c r -> p (c r)").bitcast(I32)
+        for h in range(2):
+            nc.sync.dma_start(out=xw[:, T // 2 * h : T // 2 * (h + 1)], in_=x_rows[:, T // 2 * h : T // 2 * (h + 1)])
         for q in range(4):
-            load_scales(nc.scalar if q < 2 else nc.gpsimd, xs, x_scales, q)
-
-        def deal_words(dst, src):
-            nc.vector.tensor_copy(
-                out=dst[:].rearrange("p (t m b) -> p t m b", t=PACK, b=2),
-                in_=src[:].rearrange("p (m t b) -> p t m b", t=PACK, b=2),
-            )
-
-        def deal_scales(dst, src):
-            nc.vector.tensor_copy(
-                out=dst[:].rearrange("p (t m) -> p t m", t=PACK),
-                in_=src[:].rearrange("p (m t) -> p t m", t=PACK),
-            )
-
-        w1d = keep.tile([P, 2 * H], U8, name="w1d", align_bytes=64)
-        s1d = keep.tile([P, H], U8, name="s1d", align_bytes=64)
-        deal_words(w1d, w1r)
-        deal_scales(s1d, s1r)
-
-        s2r = keep.tile([P, N], U8, name="s2r", tag="w1r", align_bytes=64)
-        nc.gpsimd.memset(s2r[:].bitcast(I32), 0)
-        for q in range(4):
+            load_scales(nc.sync, s1r, w1_scales, q)
+        for q in range(3):
             load_scales(nc.sync, s2r, w2_scales, q)
+        nc.scalar.activation(out=warm2[:], in_=warm[:], func=ACT.Tanh)
 
-        xg = keep.tile([P, S], U32, name="xg", align_bytes=64)
+        def deal_words(dst, src, ts):
+            nc.vector.tensor_copy(
+                out=dst[:].rearrange("p (t m b) -> p t m b", t=PACK, b=2)[:, ts],
+                in_=src[:].rearrange("p (m t b) -> p t m b", t=PACK, b=2)[:, ts],
+            )
+
+        def deal_scales(dst, src, ts):
+            nc.vector.tensor_copy(
+                out=dst[:].rearrange("p (t m) -> p t m", t=PACK)[:, ts, :],
+                in_=src[:].rearrange("p (m t) -> p t m", t=PACK)[:, ts, :],
+            )
+
         xgs = keep.tile([P, S], U8, name="xgs", align_bytes=64)
         nc.vector.tensor_copy(xgs[:], xs[:].indirect(offs_t[:]))
-        for h in range(2):
-            nc.vector.tensor_copy(xg[:, HALF * h : HALF * (h + 1)], xw[:].bitcast(U32).indirect(offs_t[:, 16 * h : 16 * (h + 1)]))
+        w1d = keep.tile([P, 2 * H], U8, name="w1d", tag="xs", align_bytes=64)
+        deal_words(w1d, w1r, slice(0, PACK))
+        s1d = keep.tile([P, H], U8, name="s1d", align_bytes=64)
+        xg = [keep.tile([P, HALF], U32, name="xg0", align_bytes=64)]
+        nc.vector.tensor_copy(xg[0][:], xw[:].bitcast(U32).indirect(offs_t[:, 0:16]))
+        deal_scales(s1d, s1r, slice(0, PACK))
+        xg.append(keep.tile([P, HALF], U32, name="xg1", tag="s1r", align_bytes=64))
+        nc.vector.tensor_copy(xg[1][:], xw[:].bitcast(U32).indirect(offs_t[:, 16:32]))
 
-        coef = keep.tile([P, 4, PACK], F32, name="coef")
-        for i, v in enumerate((0.35, -0.35, -0.525, 0.525)):
+        coef = keep.tile([P, 3, PACK], F32, name="coef")
+        for i, v in enumerate((0.35, -0.525, -0.175)):
             nc.gpsimd.tensor_scalar(coef[:, i, :], gain[:], v, 0.0, ALU.mult, ALU.add)
 
-        w2d = keep.tile([P, 2 * N], U8, name="w2d", tag="xw", align_bytes=64)
-        s2d = keep.tile([P, N], U8, name="s2d", align_bytes=64)
 
-        wide = [keep.tile([P, 2 * S], F32, name=f"wide{t}") for t in range(2)]
-        narrow = [keep.tile([P, S], F32, name=f"narrow{t}") for t in range(2)]
-        win = wide + narrow
+        win = [keep.tile([P, S], F32, name=f"win{t}") for t in range(PACK)]
         nb = [w[:, 0:S] for w in win]
+        th = [keep.tile([P, S], F32, name=f"th{t}") for t in range(PACK)]
         own = [keep.tile([P, S], F32, name=f"own{t}") for t in range(PACK)]
-        th23 = [keep.tile([P, S], F32, name=f"th{t}") for t in range(2)]
-        th = [w[:, S : 2 * S] for w in wide] + [x[:] for x in th23]
         sq = [keep.tile([P, S], F32, name=f"sq{t}") for t in range(PACK)]
 
-        def layer1(t, cols, name):
-            u = psum.tile([P, cols.stop - cols.start], F32, name=name, tag=name)
-            nc.tensor.matmul_mx(
-                out=u[:],
-                lhsT=w1d[:, 2 * P * t : 2 * P * (t + 1)].bitcast(FP4X4),
-                lhsT_scale=s1d[:, P * t : P * (t + 1)],
-                rhs=xg[:, cols].bitcast(FP8X4),
-                rhs_scale=xgs[:, cols],
-                start=True,
-                stop=True,
-            )
-            nc.scalar.activation(out=th[t][:, cols], in_=u[:], func=ACT.Tanh, scale=0.5)
+        def layer1(t, hs, name):
+            u = psum.tile([P, HALF * len(hs)], F32, name=name, tag=name)
+            for i, h in enumerate(hs):
+                nc.tensor.matmul_mx(
+                    out=u[:, HALF * i : HALF * (i + 1)],
+                    lhsT=w1d[:, 2 * P * t : 2 * P * (t + 1)].bitcast(FP4X4),
+                    lhsT_scale=s1d[:, P * t : P * (t + 1)],
+                    rhs=xg[h][:].bitcast(FP8X4),
+                    rhs_scale=xgs[:, HALF * h : HALF * (h + 1)],
+                    start=True,
+                    stop=True,
+                )
+            nc.scalar.activation(out=th[t][:, HALF * hs[0] : HALF * (hs[-1] + 1)], in_=u[:], func=ACT.Tanh, scale=0.5)
+
+        def square(t, cols):
             nc.scalar.activation(out=sq[t][:, cols], in_=th[t][:, cols], func=ACT.Square)
 
-        def affine_scalar(dst, t, cols, i):
-            nc.scalar.activation(out=dst[t][:, cols], in_=sq[t][:, cols], func=ACT.Identity, scale=coef[:, i, t : t + 1], bias=coef[:, i + 1, t : t + 1])
+        def make_own(t, cols):
+            nc.scalar.activation(out=own[t][:, cols], in_=sq[t][:, cols], func=ACT.Identity, scale=coef[:, 1, t : t + 1], bias=coef[:, 2, t : t + 1])
 
         halves = (slice(0, HALF), slice(HALF, S))
+        whole = slice(0, S)
         for h in range(2):
-            layer1(0, halves[h], f"bank{h}")
-            nc.vector.tensor_scalar(nb[0][:, halves[h]], sq[0][:, halves[h]], coef[:, 0, 0:1], coef[:, 1, 0:1], ALU.mult, ALU.add)
+            layer1(0, (h,), f"bank{h}")
+            nc.vector.scalar_tensor_tensor(nb[0][:, halves[h]], th[0][:, halves[h]], coef[:, 0, 0:1], th[0][:, halves[h]], ALU.mult, ALU.mult)
         for h in range(2):
-            affine_scalar(own, 0, halves[h], 2)
-        deal_words(w2d, w2r)
-        deal_scales(s2d, s2r)
+            square(0, halves[h])
+            make_own(0, halves[h])
+        s2d = keep.tile([P, N], U8, name="s2d", tag="xw", align_bytes=64)
+        deal_scales(s2d, s2r, slice(0, PACK))
+        w2d = keep.tile([P, 2 * N], U8, name="w2d", tag="s2r", align_bytes=64)
+        deal_words(w2d, w2r, slice(0, PACK))
         for t in range(1, PACK):
-            layer1(t, slice(0, S), f"bank{t + 1}")
-            affine_scalar(nb, t, slice(0, S), 0)
-            affine_scalar(own, t, slice(0, S), 2)
+            layer1(t, (0, 1), f"bank{t + 1}")
+            square(t, whole)
+            nc.scalar.activation(out=nb[t], in_=sq[t][:], func=ACT.Copy, scale=coef[:, 0, t : t + 1])
+            make_own(t, whole)
 
-        full = keep.tile([P, PACK, S], F32, name="full")
+        full = keep.tile([P, PACK, S], F32, name="full", align_bytes=64)
         parts = {}
 
         def first(t, cols, tag):
@@ -153,84 +160,71 @@ def tile_picked_cmlmap_none_po_kernel(tc, x_words, x_scales, w1_words, w1_scales
         osc = keep.tile([P, S], U8, name="osc", align_bytes=64)
         out_rows = out_0.rearrange("(p t) j -> p t j", t=PACK)
         out_w = out_1[0].rearrange("p c r -> p (c r)").bitcast(I32)
-        zb = {}
+        zb = keep.tile([P, S, PACK], BF16, name="zb", align_bytes=64)
+        ob = keep.tile([P, S, PACK], BF16, name="ob", align_bytes=64)
+        zw = keep.tile([P, S], U32, name="zw", align_bytes=64)
+        zs = keep.tile([P, S], U8, name="zs", align_bytes=64)
+        o32 = keep.tile([P, PACK, S], F32, name="o32")
         acc = {}
-        o32 = {}
-        ob = {}
 
         def blk(c):
             return slice(BLK * c, BLK * (c + 1))
 
-        def round_z(c, copy):
-            zb[c] = keep.tile([P, BLK, PACK], BF16, name=f"zb{c}", tag=f"zb{c}", align_bytes=64)
-            copy(
-                out=zb[c][:].rearrange("p (a i) t -> p a t i", i=2),
-                in_=full[:, :, blk(c)].rearrange("p t (a i) -> p a t i", i=2),
-            )
+        def weave(copy, dst, src):
+            copy(out=dst.rearrange("p (a i) t -> p a t i", i=2), in_=src.rearrange("p t (a i) -> p a t i", i=2))
+
+        def quantise(words, scales, src, cols):
+            nc.vector.quantize_mx(out=words[:, cols].bitcast(FP8X4), scales=scales[:, cols], in_=src.rearrange("p j t -> p (j t)"))
 
         def layer2(c, bank):
-            zw = keep.tile([P, BLK], U32, name=f"zw{c}", align_bytes=64)
-            zs = keep.tile([P, BLK], U8, name=f"zs{c}", align_bytes=64)
-            nc.vector.quantize_mx(out=zw[:].bitcast(FP8X4), scales=zs[:], in_=zb[c][:].rearrange("p j t -> p (j t)"))
             acc[c] = psum.tile([P, PACK, BLK], F32, name=f"acc{c}", tag=bank)
             for t in range(PACK):
                 nc.tensor.matmul_mx(
                     out=acc[c][:, t, :],
                     lhsT=w2d[:, 2 * P * t : 2 * P * (t + 1)].bitcast(FP4X4),
                     lhsT_scale=s2d[:, P * t : P * (t + 1)],
-                    rhs=zw[:].bitcast(FP8X4),
-                    rhs_scale=zs[:],
+                    rhs=zw[:, blk(c)].bitcast(FP8X4),
+                    rhs_scale=zs[:, blk(c)],
                     start=True,
                     stop=True,
                 )
 
-        def store_f32(c):
-            o32[c] = keep.tile([P, PACK, BLK], F32, name=f"o32_{c}")
-            nc.scalar.copy(out=o32[c][:], in_=acc[c][:])
-            nc.sync.dma_start(out=out_rows[:, :, blk(c)], in_=o32[c][:])
-
-        def round_out(c, copy, src):
-            ob[c] = keep.tile([P, BLK, PACK], BF16, name=f"ob{c}", align_bytes=64)
-            copy(
-                out=ob[c][:].rearrange("p (a i) t -> p a t i", i=2),
-                in_=src[:].rearrange("p t (a i) -> p a t i", i=2),
-            )
-
-        def planes(c):
-            nc.vector.quantize_mx(out=ow[:, blk(c)].bitcast(FP8X4), scales=osc[:, blk(c)], in_=ob[c][:].rearrange("p j t -> p (j t)"))
-            nc.sync.dma_start(out=out_w[:, blk(c)], in_=ow[:, blk(c)].bitcast(I32))
-
-        whole = slice(0, S)
-        first(0, whole, "p0")
-        second(0, whole)
-        first(1, whole, "p1")
-        second(1, whole)
-        first(2, halves[0], "p2")
-        second(2, halves[0])
-        first(3, halves[0], "p3")
+        for t in range(PACK - 1):
+            for h in range(2):
+                first(t, halves[h], f"p{t}{h}")
+                parts[t, h] = parts[t]
+            for h in range(2):
+                parts[t] = parts[t, h]
+                second(t, halves[h])
+        first(3, halves[0], "p30")
         second(3, blk(0))
-        round_z(0, nc.scalar.copy)
         second(3, blk(1))
-        round_z(1, nc.scalar.copy)
-        first(2, halves[1], "p3")
+        zb0 = full[:, 3, halves[1]].bitcast(BF16).rearrange("p (j t) -> p j t", t=PACK)
+        weave(nc.scalar.copy, zb0, full[:, :, blk(0)])
+        weave(nc.scalar.copy, zb[:, blk(1), :], full[:, :, blk(1)])
+        first(3, halves[1], "p31")
+        quantise(zw, zs, zb0, blk(0))
         layer2(0, "bank5")
-        second(2, halves[1])
-        first(3, halves[1], "zb0")
-        layer2(1, "bank6")
         second(3, blk(2))
-        round_z(2, nc.scalar.copy)
         second(3, blk(3))
-        round_z(3, nc.vector.tensor_copy)
+        quantise(zw, zs, zb[:, blk(1), :], blk(1))
+        layer2(1, "bank6")
+        weave(nc.scalar.copy, zb[:, blk(2), :], full[:, :, blk(2)])
+        weave(nc.vector.tensor_copy, zb[:, blk(3), :], full[:, :, blk(3)])
+        quantise(zw, zs, zb[:, blk(2), :], blk(2))
         layer2(2, "bank7")
+        quantise(zw, zs, zb[:, blk(3), :], blk(3))
         layer2(3, "bank0")
-        for c in (0, 1):
-            round_out(c, nc.scalar.copy, acc[c])
-            store_f32(c)
-            planes(c)
-        for c in (2, 3):
-            store_f32(c)
-            round_out(c, nc.vector.tensor_copy, o32[c])
-            planes(c)
+        for c in range(NBLK):
+            nc.scalar.copy(out=o32[:, :, blk(c)], in_=acc[c][:])
+            if c >= 1:
+                cols = halves[0] if c == 1 else blk(c)
+                nc.sync.dma_start(out=out_rows[:, :, cols], in_=o32[:, :, cols])
+            weave(nc.vector.tensor_copy, ob[:, blk(c), :], o32[:, :, blk(c)])
+            if c % 2:
+                quantise(ow, osc, ob[:, halves[c // 2], :], halves[c // 2])
+                eng = nc.gpsimd if c == 1 else nc.sync
+                eng.dma_start(out=out_w[:, halves[c // 2]], in_=ow[:, halves[c // 2]].bitcast(I32))
         for q in range(4):
             eng = nc.scalar if q % 2 else nc.sync
             eng.dma_start(out=out_2[0, 4 * q : 4 * q + 4, :].bitcast(I32), in_=osc[32 * q : 32 * q + 4, :].bitcast(I32))

@@ -223,8 +223,7 @@ def tile_picked_cmlmap_none_po_kernel(tc, x_words, x_scales, w1_words, w1_scales
             weave(nc.vector.tensor_copy, ob[:, blk(c), :], o32[:, :, blk(c)])
             if c % 2:
                 quantise(ow, osc, ob[:, halves[c // 2], :], halves[c // 2])
-                eng = nc.gpsimd if c == 1 else nc.sync
-                eng.dma_start(out=out_w[:, halves[c // 2]], in_=ow[:, halves[c // 2]].bitcast(I32))
+        nc.sync.dma_start(out=out_w, in_=ow[:].bitcast(I32))
         for q in range(4):
             eng = nc.scalar if q % 2 else nc.sync
             eng.dma_start(out=out_2[0, 4 * q : 4 * q + 4, :].bitcast(I32), in_=osc[32 * q : 32 * q + 4, :].bitcast(I32))

@@ -35,12 +35,10 @@ def tile_picked_cmlmap_none_po_kernel(tc, x_words, x_scales, w1_words, w1_scales
         n2_t = lists.tile([P, S // 16], U16, name="n2_t")
 
         xs = keep.tile([P, T], U8, name="xs", tag="xs", align_bytes=64)
-        w1r = keep.tile([P, 2 * H], U8, name="w1r", align_bytes=64)
-        w2r = keep.tile([P, 2 * N], U8, name="w2r", tag="w2r", align_bytes=64)
+        w1r = keep.tile([P, 2 * H], U8, name="w1r", tag="w1r", align_bytes=64)
         s1r = keep.tile([P, H], U8, name="s1r", tag="s1r", align_bytes=64)
-        s2r = keep.tile([P, N], U8, name="s2r", tag="s2r", align_bytes=64)
         gain = keep.tile([P, PACK], F32, name="gain")
-        warm = keep.tile([P, 1], F32, name="warm")
+        warm = keep.tile([P, 1], F32, name="warm", tag="warm", align_bytes=64)
         warm2 = keep.tile([P, 1], F32, name="warm2")
         blank = keep.tile([P, H // 4], I32, name="blank", tag="xw", align_bytes=64)
 
@@ -48,29 +46,26 @@ def tile_picked_cmlmap_none_po_kernel(tc, x_words, x_scales, w1_words, w1_scales
         nc.vector.memset(blank[:], 0)
         nc.vector.tensor_copy(s1r[:].bitcast(I32), blank[:])
         nc.vector.memset(warm[:], 0.0)
+        s2r = keep.tile([P, N], U8, name="s2r", tag="s2r", align_bytes=64)
         nc.vector.memset(s2r[:].bitcast(I32), 0)
         xw = keep.tile([P, T], I32, name="xw", tag="xw", align_bytes=64)
 
-        def load_scales(eng, tile, src, q):
-            eng.dma_start(out=tile[32 * q : 32 * q + 4, :].bitcast(I32), in_=src[0, 4 * q : 4 * q + 4, :].bitcast(I32))
+        def load_scales(tile, src):
+            for q in range(4):
+                nc.sync.dma_start(out=tile[32 * q : 32 * q + 4, :].bitcast(I32), in_=src[0, 4 * q : 4 * q + 4, :].bitcast(I32))
 
         nc.gpsimd.dma_start(out=w1r[:].bitcast(I32), in_=w1_words[0].bitcast(I32))
-        load_scales(nc.gpsimd, s2r, w2_scales, 3)
         nc.gpsimd.dma_start(out=gain[:], in_=gn.rearrange("(p t) o -> p (t o)", t=PACK))
-        nc.gpsimd.dma_start(out=w2r[:].bitcast(I32), in_=w2_words[0].bitcast(I32))
         nc.sync.dma_start(offs_t[:], offs)
         nc.sync.dma_start(n1_t[:], n1)
         nc.sync.dma_start(n2_t[:], n2)
-        for q in range(4):
-            load_scales(nc.sync, xs, x_scales, q)
-        x_rows = x_words[0].rearrange("p c r -> p (c r)").bitcast(I32)
-        for h in range(2):
-            nc.sync.dma_start(out=xw[:, T // 2 * h : T // 2 * (h + 1)], in_=x_rows[:, T // 2 * h : T // 2 * (h + 1)])
-        for q in range(4):
-            load_scales(nc.sync, s1r, w1_scales, q)
-        for q in range(3):
-            load_scales(nc.sync, s2r, w2_scales, q)
+        load_scales(xs, x_scales)
+        nc.sync.dma_start(out=xw[:], in_=x_words[0].rearrange("p c r -> p (c r)").bitcast(I32))
+        load_scales(s1r, w1_scales)
+        load_scales(s2r, w2_scales)
         nc.scalar.activation(out=warm2[:], in_=warm[:], func=ACT.Tanh)
+        w2r = keep.tile([P, 2 * N], U8, name="w2r", tag="warm", align_bytes=64)
+        nc.sync.dma_start(out=w2r[:].bitcast(I32), in_=w2_words[0].bitcast(I32))
 
         def deal_words(dst, src, ts):
             nc.vector.tensor_copy(
@@ -97,14 +92,16 @@ def tile_picked_cmlmap_none_po_kernel(tc, x_words, x_scales, w1_words, w1_scales
 
         coef = keep.tile([P, 3, PACK], F32, name="coef")
         for i, v in enumerate((0.35, -0.525, -0.175)):
-            nc.gpsimd.tensor_scalar(coef[:, i, :], gain[:], v, 0.0, ALU.mult, ALU.add)
+            nc.scalar.activation(out=coef[:, i, :], in_=gain[:], func=ACT.Copy, scale=v)
 
 
         win = [keep.tile([P, S], F32, name=f"win{t}") for t in range(PACK)]
         nb = [w[:, 0:S] for w in win]
         th = [keep.tile([P, S], F32, name=f"th{t}") for t in range(PACK)]
         own = [keep.tile([P, S], F32, name=f"own{t}") for t in range(PACK)]
-        sq = [keep.tile([P, S], F32, name=f"sq{t}") for t in range(PACK)]
+        full = keep.tile([P, PACK, S], F32, name="full", align_bytes=64)
+        sq = [keep.tile([P, S], F32, name=f"sq{t}") for t in range(PACK - 1)]
+        sq.append(full[:].rearrange("p t j -> p (t j)")[:, 2 * S + HALF : 3 * S + HALF])
 
         def layer1(t, hs, name):
             u = psum.tile([P, HALF * len(hs)], F32, name=name, tag=name)
@@ -141,10 +138,9 @@ def tile_picked_cmlmap_none_po_kernel(tc, x_words, x_scales, w1_words, w1_scales
         for t in range(1, PACK):
             layer1(t, (0, 1), f"bank{t + 1}")
             square(t, whole)
-            nc.scalar.activation(out=nb[t], in_=sq[t][:], func=ACT.Copy, scale=coef[:, 0, t : t + 1])
+            nc.scalar.activation(out=nb[t], in_=sq[t][:, whole], func=ACT.Copy, scale=coef[:, 0, t : t + 1])
             make_own(t, whole)
 
-        full = keep.tile([P, PACK, S], F32, name="full", align_bytes=64)
         parts = {}
 
         def first(t, cols, tag):
@@ -193,10 +189,12 @@ def tile_picked_cmlmap_none_po_kernel(tc, x_words, x_scales, w1_words, w1_scales
             for h in range(2):
                 first(t, halves[h], f"p{t}{h}")
                 parts[t, h] = parts[t]
-            for h in range(2):
+            for h in range(2 if t < 2 else 1):
                 parts[t] = parts[t, h]
                 second(t, halves[h])
         first(3, halves[0], "p30")
+        parts[2] = parts[2, 1]
+        second(2, halves[1])
         second(3, blk(0))
         second(3, blk(1))
         zb0 = full[:, 3, halves[1]].bitcast(BF16).rearrange("p (j t) -> p j t", t=PACK)

from contextlib import ExitStack

import concourse.mybir as mybir

K, T, S, N, H = 512, 2048, 512, 512, 512
FLOPS = 2 * K * H * S + 2 * H * N * S

F32 = mybir.dt.float32
BF16 = mybir.dt.bfloat16
I32 = mybir.dt.int32
U32 = mybir.dt.uint32
U16 = mybir.dt.uint16
U8 = mybir.dt.uint8
FP8X4 = mybir.dt.float8_e4m3fn_x4
FP4X4 = mybir.dt.float4_e2m1fn_x4
ACT = mybir.ActivationFunctionType
ALU = mybir.AluOpType

P = 128
PACK = 4
BLK = 128
NBLK = S // BLK
HALF = S // 2


def tile_picked_cmlmap_none_po_kernel(tc, x_words, x_scales, w1_words, w1_scales, gn, w2_words, w2_scales, offs, n1, n2, out_0, out_1, out_2):
    nc = tc.nc
    with ExitStack() as ctx:
        lists = ctx.enter_context(tc.tile_pool(name="lists", bufs=1))
        keep = ctx.enter_context(tc.tile_pool(name="keep", bufs=1))
        psum = ctx.enter_context(tc.psum_pool(name="psum", bufs=1))

        offs_t = lists.tile([P, S // 16], U16, name="offs_t")
        n1_t = lists.tile([P, S // 16], U16, name="n1_t")
        n2_t = lists.tile([P, S // 16], U16, name="n2_t")

        xs = keep.tile([P, T], U8, name="xs", tag="xs", align_bytes=64)
        w1r = keep.tile([P, 2 * H], U8, name="w1r", tag="w1r", align_bytes=64)
        s1r = keep.tile([P, H], U8, name="s1r", tag="s1r", align_bytes=64)
        gain = keep.tile([P, PACK], F32, name="gain")
        warm = keep.tile([P, 1], F32, name="warm", tag="warm", align_bytes=64)
        warm2 = keep.tile([P, 1], F32, name="warm2")
        blank = keep.tile([P, H // 4], I32, name="blank", tag="xw", align_bytes=64)

        nc.vector.memset(xs[:].bitcast(I32), 0)
        nc.vector.memset(blank[:], 0)
        nc.vector.tensor_copy(s1r[:].bitcast(I32), blank[:])
        nc.vector.memset(warm[:], 0.0)
        s2r = keep.tile([P, N], U8, name="s2r", tag="s2r", align_bytes=64)
        nc.vector.memset(s2r[:].bitcast(I32), 0)
        xw = keep.tile([P, T], I32, name="xw", tag="xw", align_bytes=64)

        def load_scales(tile, src):
            for q in range(4):
                nc.sync.dma_start(out=tile[32 * q : 32 * q + 4, :].bitcast(I32), in_=src[0, 4 * q : 4 * q + 4, :].bitcast(I32))

        nc.gpsimd.dma_start(out=w1r[:].bitcast(I32), in_=w1_words[0].bitcast(I32))
        nc.gpsimd.dma_start(out=gain[:], in_=gn.rearrange("(p t) o -> p (t o)", t=PACK))
        nc.sync.dma_start(offs_t[:], offs)
        nc.sync.dma_start(n1_t[:], n1)
        nc.sync.dma_start(n2_t[:], n2)
        load_scales(xs, x_scales)
        nc.sync.dma_start(out=xw[:], in_=x_words[0].rearrange("p c r -> p (c r)").bitcast(I32))
        load_scales(s1r, w1_scales)
        load_scales(s2r, w2_scales)
        nc.scalar.activation(out=warm2[:], in_=warm[:], func=ACT.Tanh)
        w2r = keep.tile([P, 2 * N], U8, name="w2r", tag="warm", align_bytes=64)
        nc.sync.dma_start(out=w2r[:].bitcast(I32), in_=w2_words[0].bitcast(I32))

        def deal_words(dst, src, ts):
            nc.vector.tensor_copy(
                out=dst[:].rearrange("p (t m b) -> p t m b", t=PACK, b=2)[:, ts],
                in_=src[:].rearrange("p (m t b) -> p t m b", t=PACK, b=2)[:, ts],
            )

        def deal_scales(dst, src, ts):
            nc.vector.tensor_copy(
                out=dst[:].rearrange("p (t m) -> p t m", t=PACK)[:, ts, :],
                in_=src[:].rearrange("p (m t) -> p t m", t=PACK)[:, ts, :],
            )

        xgs = keep.tile([P, S], U8, name="xgs", align_bytes=64)
        nc.vector.tensor_copy(xgs[:], xs[:].indirect(offs_t[:]))
        w1d = keep.tile([P, 2 * H], U8, name="w1d", tag="xs", align_bytes=64)
        deal_words(w1d, w1r, slice(0, PACK))
        s1d = keep.tile([P, H], U8, name="s1d", align_bytes=64)
        xg = [keep.tile([P, HALF], U32, name="xg0", align_bytes=64)]
        nc.vector.tensor_copy(xg[0][:], xw[:].bitcast(U32).indirect(offs_t[:, 0:16]))
        deal_scales(s1d, s1r, slice(0, PACK))
        xg.append(keep.tile([P, HALF], U32, name="xg1", tag="s1r", align_bytes=64))
        nc.vector.tensor_copy(xg[1][:], xw[:].bitcast(U32).indirect(offs_t[:, 16:32]))

        coef = keep.tile([P, 3, PACK], F32, name="coef")
        for i, v in enumerate((0.35, -0.525, -0.175)):
            nc.scalar.activation(out=coef[:, i, :], in_=gain[:], func=ACT.Copy, scale=v)


        win = [keep.tile([P, S], F32, name=f"win{t}") for t in range(PACK)]
        nb = [w[:, 0:S] for w in win]
        th = [keep.tile([P, S], F32, name=f"th{t}") for t in range(PACK)]
        own = [keep.tile([P, S], F32, name=f"own{t}") for t in range(PACK)]
        full = keep.tile([P, PACK, S], F32, name="full", align_bytes=64)
        sq = [keep.tile([P, S], F32, name=f"sq{t}") for t in range(PACK - 1)]
        sq.append(full[:].rearrange("p t j -> p (t j)")[:, 2 * S + HALF : 3 * S + HALF])

        def layer1(t, hs, name):
            u = psum.tile([P, HALF * len(hs)], F32, name=name, tag=name)
            for i, h in enumerate(hs):
                nc.tensor.matmul_mx(
                    out=u[:, HALF * i : HALF * (i + 1)],
                    lhsT=w1d[:, 2 * P * t : 2 * P * (t + 1)].bitcast(FP4X4),
                    lhsT_scale=s1d[:, P * t : P * (t + 1)],
                    rhs=xg[h][:].bitcast(FP8X4),
                    rhs_scale=xgs[:, HALF * h : HALF * (h + 1)],
                    start=True,
                    stop=True,
                )
            nc.scalar.activation(out=th[t][:, HALF * hs[0] : HALF * (hs[-1] + 1)], in_=u[:], func=ACT.Tanh, scale=0.5)

        def square(t, cols):
            nc.scalar.activation(out=sq[t][:, cols], in_=th[t][:, cols], func=ACT.Square)

        def make_own(t, cols):
            nc.scalar.activation(out=own[t][:, cols], in_=sq[t][:, cols], func=ACT.Identity, scale=coef[:, 1, t : t + 1], bias=coef[:, 2, t : t + 1])

        halves = (slice(0, HALF), slice(HALF, S))
        whole = slice(0, S)
        for h in range(2):
            layer1(0, (h,), f"bank{h}")
            nc.vector.scalar_tensor_tensor(nb[0][:, halves[h]], th[0][:, halves[h]], coef[:, 0, 0:1], th[0][:, halves[h]], ALU.mult, ALU.mult)
        for h in range(2):
            square(0, halves[h])
            make_own(0, halves[h])
        s2d = keep.tile([P, N], U8, name="s2d", tag="xw", align_bytes=64)
        deal_scales(s2d, s2r, slice(0, PACK))
        w2d = keep.tile([P, 2 * N], U8, name="w2d", tag="s2r", align_bytes=64)
        deal_words(w2d, w2r, slice(0, PACK))
        for t in range(1, PACK):
            layer1(t, (0, 1), f"bank{t + 1}")
            square(t, whole)
            nc.scalar.activation(out=nb[t], in_=sq[t][:, whole], func=ACT.Copy, scale=coef[:, 0, t : t + 1])
            make_own(t, whole)

        parts = {}

        def first(t, cols, tag):
            dst = keep.tile([P, cols.stop - cols.start], F32, name=f"part{t}_{cols.start}", tag=tag, align_bytes=64)
            parts[t] = (dst, cols.start)
            nc.vector.tensor_tensor(dst[:], win[t][:].indirect(n1_t[:, cols.start // 16 : cols.stop // 16]), own[t][:, cols], ALU.add)

        def second(t, cols):
            src, base = parts[t]
            nc.vector.tensor_tensor(full[:, t, cols], win[t][:].indirect(n2_t[:, cols.start // 16 : cols.stop // 16]), src[:, cols.start - base : cols.stop - base], ALU.add)

        ow = keep.tile([P, S], U32, name="ow", align_bytes=64)
        osc = keep.tile([P, S], U8, name="osc", align_bytes=64)
        out_rows = out_0.rearrange("(p t) j -> p t j", t=PACK)
        out_w = out_1[0].rearrange("p c r -> p (c r)").bitcast(I32)
        zb = keep.tile([P, S, PACK], BF16, name="zb", align_bytes=64)
        ob = keep.tile([P, S, PACK], BF16, name="ob", align_bytes=64)
        zw = keep.tile([P, S], U32, name="zw", align_bytes=64)
        zs = keep.tile([P, S], U8, name="zs", align_bytes=64)
        o32 = keep.tile([P, PACK, S], F32, name="o32")
        acc = {}

        def blk(c):
            return slice(BLK * c, BLK * (c + 1))

        def weave(copy, dst, src):
            copy(out=dst.rearrange("p (a i) t -> p a t i", i=2), in_=src.rearrange("p t (a i) -> p a t i", i=2))

        def quantise(words, scales, src, cols):
            nc.vector.quantize_mx(out=words[:, cols].bitcast(FP8X4), scales=scales[:, cols], in_=src.rearrange("p j t -> p (j t)"))

        def layer2(c, bank):
            acc[c] = psum.tile([P, PACK, BLK], F32, name=f"acc{c}", tag=bank)
            for t in range(PACK):
                nc.tensor.matmul_mx(
                    out=acc[c][:, t, :],
                    lhsT=w2d[:, 2 * P * t : 2 * P * (t + 1)].bitcast(FP4X4),
                    lhsT_scale=s2d[:, P * t : P * (t + 1)],
                    rhs=zw[:, blk(c)].bitcast(FP8X4),
                    rhs_scale=zs[:, blk(c)],
                    start=True,
                    stop=True,
                )

        for t in range(PACK - 1):
            for h in range(2):
                first(t, halves[h], f"p{t}{h}")
                parts[t, h] = parts[t]
            for h in range(2 if t < 2 else 1):
                parts[t] = parts[t, h]
                second(t, halves[h])
        first(3, halves[0], "p30")
        parts[2] = parts[2, 1]
        second(2, halves[1])
        second(3, blk(0))
        second(3, blk(1))
        zb0 = full[:, 3, halves[1]].bitcast(BF16).rearrange("p (j t) -> p j t", t=PACK)
        weave(nc.scalar.copy, zb0, full[:, :, blk(0)])
        weave(nc.scalar.copy, zb[:, blk(1), :], full[:, :, blk(1)])
        first(3, halves[1], "p31")
        quantise(zw, zs, zb0, blk(0))
        layer2(0, "bank5")
        second(3, blk(2))
        second(3, blk(3))
        quantise(zw, zs, zb[:, blk(1), :], blk(1))
        layer2(1, "bank6")
        weave(nc.scalar.copy, zb[:, blk(2), :], full[:, :, blk(2)])
        weave(nc.vector.tensor_copy, zb[:, blk(3), :], full[:, :, blk(3)])
        quantise(zw, zs, zb[:, blk(2), :], blk(2))
        layer2(2, "bank7")
        quantise(zw, zs, zb[:, blk(3), :], blk(3))
        layer2(3, "bank0")
        for c in range(NBLK):
            nc.scalar.copy(out=o32[:, :, blk(c)], in_=acc[c][:])
            if c >= 1:
                cols = halves[0] if c == 1 else blk(c)
                nc.sync.dma_start(out=out_rows[:, :, cols], in_=o32[:, :, cols])
            weave(nc.vector.tensor_copy, ob[:, blk(c), :], o32[:, :, blk(c)])
            if c % 2:
                quantise(ow, osc, ob[:, halves[c // 2], :], halves[c // 2])
        nc.sync.dma_start(out=out_w, in_=ow[:].bitcast(I32))
        for q in range(4):
            eng = nc.scalar if q % 2 else nc.sync
            eng.dma_start(out=out_2[0, 4 * q : 4 * q + 4, :].bitcast(I32), in_=osc[32 * q : 32 * q + 4, :].bitcast(I32))
